import numpy as np
import ml_dtypes


def mxq(x, axis, fmt="e4m3"):
    dtype, down = {"e4m3": (ml_dtypes.float8_e4m3fn, 7), "e5m2": (ml_dtypes.float8_e5m2, 14)}[fmt]
    v = np.moveaxis(np.asarray(x, np.float32).astype(ml_dtypes.bfloat16).astype(np.float64), axis, -1)
    blocks = v.reshape(v.shape[:-1] + (-1, 32))
    amax = np.abs(blocks).max(-1, keepdims=True)
    byte = np.maximum(np.where(amax > 0, np.frexp(amax)[1] - 1 + 127, 0) - down, 1)
    scale = np.exp2(byte - 127.0)
    codes = (blocks / scale).astype(np.float32).astype(dtype).astype(np.float64)
    return np.moveaxis((codes * scale).reshape(v.shape), -1, axis)


WIDE = False


def mx_kscale(k):
    if not WIDE:
        return np.ones(k)
    levels = np.array([10, -10, 5, -5, 0])
    if k % 512:
        return np.exp2(np.random.permutation(np.resize(levels, k // 32))).repeat(32)
    a = np.empty((k // 512, 16))
    for p in range(k // 512):
        a[p, :8] = np.random.permutation(np.resize(levels, 8))
        for g in range(8):
            far = levels[np.abs(levels - a[p, g]) >= 10]
            a[p, g + 8] = far[np.random.randint(len(far))]
    return np.exp2(a.ravel()).repeat(32)


def f64(x):
    return np.asarray(x).astype(np.float64)


def striped(idx):
    return np.tile(idx.reshape(-1, 16).T, (8, 1)).astype(np.uint16)


def unstriped(offs):
    return offs[:16].T.reshape(-1).astype(np.int64)


def pack_weight(w):
    k, n = w.shape
    w = f64(np.asarray(w, np.float32).astype(ml_dtypes.bfloat16)).reshape(k // 32, 32, n)
    amax = np.abs(w).max(1)
    byte = np.clip(np.where(amax > 0, np.frexp(amax)[1] - 1 + 127 - 7, 1), 1, 254)
    scaled = (w * np.exp2(127.0 - byte)[:, None, :]).reshape(k, n).astype(np.float32)
    words = np.ascontiguousarray(scaled.reshape(k // 512, 128, 4, n).transpose(0, 1, 3, 2)).astype(ml_dtypes.float8_e4m3fn).view(np.uint8)
    return words, np.ascontiguousarray(byte.astype(np.uint8).reshape(k // 512, 16, n))


def unpack_weight(words, scales):
    g, p, n, _ = words.shape
    vals = np.ascontiguousarray(words).view(ml_dtypes.float8_e4m3fn).astype(np.float64) * np.repeat(np.exp2(scales.astype(np.float64) - 127.0), 8, axis=1)[..., None]
    return vals.transpose(0, 1, 3, 2).reshape(g * 512, n)


def gelu(v):
    return 0.5 * v * (1.0 + np.tanh(np.sqrt(2.0 / np.pi) * (v + 0.044715 * v**3)))


K, T, S, N = 1024, 2048, 1024, 256


def setup_inputs():
    n = np.random.standard_normal
    s = mx_kscale(K)[:, None]
    words, scales = pack_weight(n((K, N)) / np.sqrt(K) / s)
    return {
        "xT": (n((K, S)) * s).astype(np.float32),
        "w_words": words,
        "w_scales": scales,
        "b": (0.3 * n((N, 1))).astype(np.float32),
        "gate": np.tile(np.random.uniform(0.2, 1.0, S), (N, 1)).astype(np.float32),
        "offs": striped(np.sort(np.random.permutation(T)[:S])),
    }


def reference(xT, w_words, w_scales, b, gate, offs):
    w = unpack_weight(w_words, w_scales)
    idx = unstriped(offs)
    xq = mxq(f64(xT), 0, "e4m3")
    y = w.T @ xq
    y = gelu(y + f64(b))
    out = np.zeros((N, T))
    out[:, idx] = f64(gate) * y
    return out

@@ -1,0 +1,137 @@
+from contextlib import ExitStack
+
+import concourse.mybir as mybir
+
+K, S, N, T = 1024, 1024, 256, 2048
+FLOPS = 2 * K * S * N
+
+F32 = mybir.dt.float32
+BF16 = mybir.dt.bfloat16
+I32 = mybir.dt.int32
+U32 = mybir.dt.uint32
+U16 = mybir.dt.uint16
+U8 = mybir.dt.uint8
+FP8X4 = mybir.dt.float8_e4m3fn_x4
+MULT = mybir.AluOpType.mult
+GELU = mybir.ActivationFunctionType.Gelu_apprx_tanh
+
+P = 128
+PACK = 4
+K_PASS = P * PACK
+PASSES = K // K_PASS
+M_TILES = N // P
+
+LOADS = ((0, 0, 512, 160), (1, 0, 512, 160), (0, 512, 512, 160), (1, 512, 256, 128), (1, 768, 256, 176))
+BLOCKS = ((0, 512), (512, 256), (768, 256))
+
+
+def tile_picked_place_lin_gelu_srt_l_kernel(tc, xT, w_words, w_scales, b, gate, offs, out):
+    nc = tc.nc
+    with ExitStack() as ctx:
+        keep = ctx.enter_context(tc.tile_pool(name="keep", bufs=1))
+        psum = ctx.enter_context(tc.psum_pool(name="psum", bufs=1))
+
+        offsets = keep.tile([P, S // 16], U16, name="offsets")
+        w_codes = keep.tile([P, PASSES, N], U32, name="w_codes", align_bytes=64)
+        w_planes = keep.tile([P, PASSES, N], U8, name="w_planes", align_bytes=64)
+        warm = keep.tile([P, 1], F32, name="warm")
+        warmed = keep.tile([P, 1], F32, name="warmed")
+
+        raws = []
+        for i, (k, t0, width, v) in enumerate(LOADS):
+            raw = keep.tile([P, PACK, width], F32, name=f"raw{i}", align_bytes=64)
+            raws.append(raw)
+        gates = []
+        for h in range(2):
+            gate_half = keep.tile([P, M_TILES, S // 2], F32, name=f"gate{h}", align_bytes=64)
+            gates.append(gate_half)
+
+        def load_x(i):
+            k, t0, width, v = LOADS[i]
+            rows = xT[k * K_PASS : (k + 1) * K_PASS, t0 : t0 + width]
+            nc.sync.dma_start(out=raws[i][:], in_=rows.rearrange("(p j) w -> p j w", j=PACK))
+
+        def load_gate(h):
+            cols = gate[:, h * (S // 2) : (h + 1) * (S // 2)]
+            nc.sync.dma_start(out=gates[h][:], in_=cols.rearrange("(m p) w -> p m w", p=P))
+
+        load_x(0)
+        nc.vector.memset(w_planes[:].rearrange("p a n -> p (a n)").bitcast(I32), 0)
+        nc.vector.memset(warm[:], 0.0)
+        biases = []
+        for m in range(M_TILES):
+            bias = keep.tile([P, 1], F32, name=f"bias{m}")
+            nc.scalar.dma_start(out=bias[:], in_=b[m * P : (m + 1) * P, :])
+            biases.append(bias)
+        for q in range(4):
+            nc.scalar.dma_start(
+                out=w_planes[32 * q : 32 * q + 4].bitcast(I32),
+                in_=w_scales[:, 4 * q : 4 * q + 4, :].rearrange("a q n -> q a n").bitcast(I32),
+            )
+        nc.scalar.activation(out=warmed[:], in_=warm[:], func=GELU)
+        nc.sync.dma_start(out=w_codes[:].bitcast(I32), in_=w_words.rearrange("a p n r -> p a (n r)").bitcast(I32))
+        load_x(1)
+        nc.sync.dma_start(offsets[:], offs)
+        load_gate(0)
+        for i in range(2, len(LOADS)):
+            load_x(i)
+        load_gate(1)
+
+        windows = []
+        for m in range(M_TILES):
+            window = keep.tile([P, T], F32, name=f"window{m}", align_bytes=64)
+            nc.vector.memset(window[:], 0.0)
+            windows.append(window)
+
+        operands = {}
+
+        def quantize(i):
+            k, t0, width, v = LOADS[i]
+            grouped = keep.tile([P, width, PACK], BF16, name=f"grouped{i}", align_bytes=64)
+            codes = keep.tile([P, width], U32, name=f"codes{i}", align_bytes=64)
+            planes = keep.tile([P, width], U8, name=f"planes{i}", align_bytes=64)
+            turned = raws[i][:].rearrange("p j w -> p w j")
+            nc.scalar.copy(out=grouped[:, v:, :], in_=turned[:, v:, :])
+            nc.vector.tensor_copy(out=grouped[:, :v, :], in_=turned[:, :v, :])
+            nc.vector.quantize_mx(
+                out=codes[:].bitcast(FP8X4), scales=planes[:], in_=grouped[:].rearrange("p w j -> p (w j)")
+            )
+            operands[i] = (k, t0, width, codes, planes)
+
+        def block(n):
+            t0, width = BLOCKS[n]
+            for m in range(M_TILES):
+                acc = psum.tile([P, width], F32, name=f"acc{n}_{m}")
+                m_cols = slice(m * P, (m + 1) * P)
+                used = [o for o in operands.values() if o[1] <= t0 and t0 + width <= o[1] + o[2]]
+                for a, (k, x0, x_width, codes, planes) in enumerate(used):
+                    cols = slice(t0 - x0, t0 - x0 + width)
+                    nc.tensor.matmul_mx(
+                        out=acc[:],
+                        lhsT=w_codes[:, k, m_cols].bitcast(FP8X4),
+                        lhsT_scale=w_planes[:, k, m_cols],
+                        rhs=codes[:, cols].bitcast(FP8X4),
+                        rhs_scale=planes[:, cols],
+                        start=(a == 0),
+                        stop=(a == len(used) - 1),
+                    )
+                y = keep.tile([P, width], F32, name=f"y{n}_{m}", align_bytes=64)
+                nc.scalar.activation(out=y[:], in_=acc[:], func=GELU, bias=biases[m][:])
+                h, g0 = divmod(t0, S // 2)
+                nc.vector.tensor_tensor(
+                    windows[m][:].indirect(offsets[:, t0 // 16 : (t0 + width) // 16]),
+                    y[:],
+                    gates[h][:, m, g0 : g0 + width],
+                    MULT,
+                )
+
+        quantize(0)
+        quantize(1)
+        block(0)
+        quantize(2)
+        quantize(3)
+        block(1)
+        quantize(4)
+        block(2)
+        for m in range(M_TILES):
+            nc.sync.dma_start(out=out[m * P : (m + 1) * P, :], in_=windows[m][:])

@@ -20,8 +20,9 @@ PACK = 4
 K_PASS = P * PACK
 PASSES = K // K_PASS
 M_TILES = N // P
+HALF = S // 2
 
-LOADS = ((0, 0, 512, 160), (1, 0, 512, 160), (0, 512, 512, 160), (1, 512, 256, 128), (1, 768, 256, 176))
+LOADS = ((0, 0, 512, 224), (1, 0, 512, 224), (0, 512, 512, 160), (1, 512, 256, 128), (1, 768, 256, 176))
 BLOCKS = ((0, 512), (512, 256), (768, 256))
 
 
@@ -36,54 +37,56 @@ def tile_picked_place_lin_gelu_srt_l_kernel(tc, xT, w_words, w_scales, b, gate, 
         w_planes = keep.tile([P, PASSES, N], U8, name="w_planes", align_bytes=64)
         warm = keep.tile([P, 1], F32, name="warm")
         warmed = keep.tile([P, 1], F32, name="warmed")
-
         raws = []
         for i, (k, t0, width, v) in enumerate(LOADS):
             raw = keep.tile([P, PACK, width], F32, name=f"raw{i}", align_bytes=64)
             raws.append(raw)
-        gates = []
-        for h in range(2):
-            gate_half = keep.tile([P, M_TILES, S // 2], F32, name=f"gate{h}", align_bytes=64)
-            gates.append(gate_half)
+        gate0 = keep.tile([P, S], F32, name="gate0", align_bytes=64)
+        gate1a = keep.tile([P, HALF], F32, name="gate1a", align_bytes=64)
+        gate1b = keep.tile([P, HALF], F32, name="gate1b", align_bytes=64)
 
         def load_x(i):
             k, t0, width, v = LOADS[i]
             rows = xT[k * K_PASS : (k + 1) * K_PASS, t0 : t0 + width]
             nc.sync.dma_start(out=raws[i][:], in_=rows.rearrange("(p j) w -> p j w", j=PACK))
 
-        def load_gate(h):
-            cols = gate[:, h * (S // 2) : (h + 1) * (S // 2)]
-            nc.sync.dma_start(out=gates[h][:], in_=cols.rearrange("(m p) w -> p m w", p=P))
-
         load_x(0)
+        nc.sync.dma_start(out=w_codes[:].bitcast(I32), in_=w_words.rearrange("a p n r -> p a (n r)").bitcast(I32))
+        load_x(1)
         nc.vector.memset(w_planes[:].rearrange("p a n -> p (a n)").bitcast(I32), 0)
-        nc.vector.memset(warm[:], 0.0)
-        biases = []
-        for m in range(M_TILES):
-            bias = keep.tile([P, 1], F32, name=f"bias{m}")
-            nc.scalar.dma_start(out=bias[:], in_=b[m * P : (m + 1) * P, :])
-            biases.append(bias)
         for q in range(4):
             nc.scalar.dma_start(
                 out=w_planes[32 * q : 32 * q + 4].bitcast(I32),
                 in_=w_scales[:, 4 * q : 4 * q + 4, :].rearrange("a q n -> q a n").bitcast(I32),
             )
-        nc.scalar.activation(out=warmed[:], in_=warm[:], func=GELU)
-        nc.sync.dma_start(out=w_codes[:].bitcast(I32), in_=w_words.rearrange("a p n r -> p a (n r)").bitcast(I32))
-        load_x(1)
         nc.sync.dma_start(offsets[:], offs)
-        load_gate(0)
-        for i in range(2, len(LOADS)):
-            load_x(i)
-        load_gate(1)
+        nc.sync.dma_start(out=gate0[:], in_=gate[0:P, :])
+        nc.sync.dma_start(out=gate1a[:], in_=gate[P:N, 0:HALF])
+        load_x(2)
+        load_x(3)
+        load_x(4)
+        nc.sync.dma_start(out=gate1b[:], in_=gate[P:N, HALF:S])
 
+        biases = []
+        for m in range(M_TILES):
+            bias = keep.tile([P, 1], F32, name=f"bias{m}")
+            nc.gpsimd.dma_start(out=bias[:], in_=b[m * P : (m + 1) * P, :])
+            biases.append(bias)
+
+        nc.vector.memset(warm[:], 0.0)
+        nc.scalar.activation(out=warmed[:], in_=warm[:], func=GELU)
         windows = []
         for m in range(M_TILES):
             window = keep.tile([P, T], F32, name=f"window{m}", align_bytes=64)
             nc.vector.memset(window[:], 0.0)
             windows.append(window)
 
-        operands = {}
+        accs = {}
+        ys = {}
+        for n, (t0, width) in enumerate(BLOCKS):
+            for m in range(M_TILES):
+                accs[n, m] = psum.tile([P, width], F32, name=f"acc{n}_{m}")
+                ys[n, m] = keep.tile([P, width], F32, name=f"y{n}_{m}", align_bytes=64)
 
         def quantize(i):
             k, t0, width, v = LOADS[i]
@@ -96,42 +99,45 @@ def tile_picked_place_lin_gelu_srt_l_kernel(tc, xT, w_words, w_scales, b, gate, 
             nc.vector.quantize_mx(
                 out=codes[:].bitcast(FP8X4), scales=planes[:], in_=grouped[:].rearrange("p w j -> p (w j)")
             )
-            operands[i] = (k, t0, width, codes, planes)
+            for n, (b0, b_width) in enumerate(BLOCKS):
+                if t0 <= b0 and b0 + b_width <= t0 + width:
+                    cols = slice(b0 - t0, b0 - t0 + b_width)
+                    for m in range(M_TILES):
+                        m_cols = slice(m * P, (m + 1) * P)
+                        nc.tensor.matmul_mx(
+                            out=accs[n, m][:],
+                            lhsT=w_codes[:, k, m_cols].bitcast(FP8X4),
+                            lhsT_scale=w_planes[:, k, m_cols],
+                            rhs=codes[:, cols].bitcast(FP8X4),
+                            rhs_scale=planes[:, cols],
+                            start=(k == 0),
+                            stop=(k == PASSES - 1),
+                        )
 
-        def block(n):
-            t0, width = BLOCKS[n]
+        def activate(n):
             for m in range(M_TILES):
-                acc = psum.tile([P, width], F32, name=f"acc{n}_{m}")
-                m_cols = slice(m * P, (m + 1) * P)
-                used = [o for o in operands.values() if o[1] <= t0 and t0 + width <= o[1] + o[2]]
-                for a, (k, x0, x_width, codes, planes) in enumerate(used):
-                    cols = slice(t0 - x0, t0 - x0 + width)
-                    nc.tensor.matmul_mx(
-                        out=acc[:],
-                        lhsT=w_codes[:, k, m_cols].bitcast(FP8X4),
-                        lhsT_scale=w_planes[:, k, m_cols],
-                        rhs=codes[:, cols].bitcast(FP8X4),
-                        rhs_scale=planes[:, cols],
-                        start=(a == 0),
-                        stop=(a == len(used) - 1),
-                    )
-                y = keep.tile([P, width], F32, name=f"y{n}_{m}", align_bytes=64)
-                nc.scalar.activation(out=y[:], in_=acc[:], func=GELU, bias=biases[m][:])
-                h, g0 = divmod(t0, S // 2)
-                nc.vector.tensor_tensor(
-                    windows[m][:].indirect(offsets[:, t0 // 16 : (t0 + width) // 16]),
-                    y[:],
-                    gates[h][:, m, g0 : g0 + width],
-                    MULT,
-                )
+                nc.scalar.activation(out=ys[n, m][:], in_=accs[n, m][:], func=GELU, bias=biases[m][:])
+
+        def scatter(n, m):
+            t0, width = BLOCKS[n]
+            weight = gate0[:, t0 : t0 + width] if m == 0 else (gate1a[:, t0 : t0 + width] if t0 < HALF else gate1b[:, t0 - HALF : t0 - HALF + width])
+            nc.vector.tensor_tensor(
+                windows[m][:].indirect(offsets[:, t0 // 16 : (t0 + width) // 16]), ys[n, m][:], weight, MULT
+            )
 
         quantize(0)
         quantize(1)
-        block(0)
+        activate(0)
+        scatter(0, 0)
         quantize(2)
         quantize(3)
-        block(1)
+        activate(1)
+        scatter(0, 1)
         quantize(4)
-        block(2)
-        for m in range(M_TILES):
-            nc.sync.dma_start(out=out[m * P : (m + 1) * P, :], in_=windows[m][:])
+        activate(2)
+        scatter(1, 0)
+        scatter(2, 0)
+        nc.sync.dma_start(out=out[0:P, :], in_=windows[0][:])
+        scatter(1, 1)
+        scatter(2, 1)
+        nc.sync.dma_start(out=out[P:N, :], in_=windows[1][:])

@@ -20,10 +20,19 @@ PACK = 4
 K_PASS = P * PACK
 PASSES = K // K_PASS
 M_TILES = N // P
-HALF = S // 2
 
-LOADS = ((0, 0, 512, 224), (1, 0, 512, 224), (0, 512, 512, 160), (1, 512, 256, 128), (1, 768, 256, 176))
-BLOCKS = ((0, 512), (512, 256), (768, 256))
+LOADS = (
+    (0, 0, 256, 128),
+    (1, 0, 256, 128),
+    (0, 256, 256, 32),
+    (1, 256, 256, 32),
+    (0, 512, 256, 32),
+    (1, 512, 256, 32),
+    (0, 768, 256, 32),
+    (1, 768, 256, 128),
+)
+BLOCKS = ((0, 256), (256, 256), (512, 256), (768, 256))
+GATES = ((0, 256), (256, 256), (512, 512))
 
 
 def tile_picked_place_lin_gelu_srt_l_kernel(tc, xT, w_words, w_scales, b, gate, offs, out):
@@ -41,37 +50,42 @@ def tile_picked_place_lin_gelu_srt_l_kernel(tc, xT, w_words, w_scales, b, gate, 
         for i, (k, t0, width, v) in enumerate(LOADS):
             raw = keep.tile([P, PACK, width], F32, name=f"raw{i}", align_bytes=64)
             raws.append(raw)
-        gate0 = keep.tile([P, S], F32, name="gate0", align_bytes=64)
-        gate1a = keep.tile([P, HALF], F32, name="gate1a", align_bytes=64)
-        gate1b = keep.tile([P, HALF], F32, name="gate1b", align_bytes=64)
+        gates = []
+        for h, (t0, width) in enumerate(GATES):
+            gate_part = keep.tile([P, M_TILES, width], F32, name=f"gate{h}", align_bytes=64)
+            gates.append(gate_part)
+        nc.gpsimd.memset(w_planes[:].rearrange("p a n -> p (a n)").bitcast(I32), 0)
 
         def load_x(i):
             k, t0, width, v = LOADS[i]
             rows = xT[k * K_PASS : (k + 1) * K_PASS, t0 : t0 + width]
             nc.sync.dma_start(out=raws[i][:], in_=rows.rearrange("(p j) w -> p j w", j=PACK))
 
+        def load_gate(h):
+            cols = gate[:, GATES[h][0] : GATES[h][0] + GATES[h][1]]
+            nc.sync.dma_start(out=gates[h][:], in_=cols.rearrange("(m p) w -> p m w", p=P))
+
         load_x(0)
-        nc.sync.dma_start(out=w_codes[:].bitcast(I32), in_=w_words.rearrange("a p n r -> p a (n r)").bitcast(I32))
-        load_x(1)
-        nc.vector.memset(w_planes[:].rearrange("p a n -> p (a n)").bitcast(I32), 0)
         for q in range(4):
             nc.scalar.dma_start(
                 out=w_planes[32 * q : 32 * q + 4].bitcast(I32),
                 in_=w_scales[:, 4 * q : 4 * q + 4, :].rearrange("a q n -> q a n").bitcast(I32),
             )
+        bias = keep.tile([P, M_TILES], F32, name="bias")
+        with nc.allow_non_contiguous_dma(reason="one bias value for each partition and output tile"):
+            nc.scalar.dma_start(out=bias[:], in_=b.rearrange("(m p) o -> p (m o)", p=P))
+        nc.sync.dma_start(out=w_codes[:].bitcast(I32), in_=w_words.rearrange("a p n r -> p a (n r)").bitcast(I32))
+        load_x(1)
         nc.sync.dma_start(offsets[:], offs)
-        nc.sync.dma_start(out=gate0[:], in_=gate[0:P, :])
-        nc.sync.dma_start(out=gate1a[:], in_=gate[P:N, 0:HALF])
+        load_gate(0)
         load_x(2)
         load_x(3)
+        load_gate(1)
         load_x(4)
-        nc.sync.dma_start(out=gate1b[:], in_=gate[P:N, HALF:S])
-
-        biases = []
-        for m in range(M_TILES):
-            bias = keep.tile([P, 1], F32, name=f"bias{m}")
-            nc.gpsimd.dma_start(out=bias[:], in_=b[m * P : (m + 1) * P, :])
-            biases.append(bias)
+        load_x(5)
+        load_x(6)
+        load_x(7)
+        load_gate(2)
 
         nc.vector.memset(warm[:], 0.0)
         nc.scalar.activation(out=warmed[:], in_=warm[:], func=GELU)
@@ -93,9 +107,10 @@ def tile_picked_place_lin_gelu_srt_l_kernel(tc, xT, w_words, w_scales, b, gate, 
             grouped = keep.tile([P, width, PACK], BF16, name=f"grouped{i}", align_bytes=64)
             codes = keep.tile([P, width], U32, name=f"codes{i}", align_bytes=64)
             planes = keep.tile([P, width], U8, name=f"planes{i}", align_bytes=64)
-            turned = raws[i][:].rearrange("p j w -> p w j")
-            nc.scalar.copy(out=grouped[:, v:, :], in_=turned[:, v:, :])
-            nc.vector.tensor_copy(out=grouped[:, :v, :], in_=turned[:, :v, :])
+            turned = raws[i][:].rearrange("p j (c i) -> p c j i", i=4)
+            laid = grouped[:].rearrange("p (c i) j -> p c j i", i=4)
+            nc.scalar.copy(out=laid[:, v // 4 :], in_=turned[:, v // 4 :])
+            nc.vector.tensor_copy(out=laid[:, : v // 4], in_=turned[:, : v // 4])
             nc.vector.quantize_mx(
                 out=codes[:].bitcast(FP8X4), scales=planes[:], in_=grouped[:].rearrange("p w j -> p (w j)")
             )
@@ -116,11 +131,13 @@ def tile_picked_place_lin_gelu_srt_l_kernel(tc, xT, w_words, w_scales, b, gate, 
 
         def activate(n):
             for m in range(M_TILES):
-                nc.scalar.activation(out=ys[n, m][:], in_=accs[n, m][:], func=GELU, bias=biases[m][:])
+                nc.scalar.activation(out=ys[n, m][:], in_=accs[n, m][:], func=GELU, bias=bias[:, m : m + 1])
 
         def scatter(n, m):
             t0, width = BLOCKS[n]
-            weight = gate0[:, t0 : t0 + width] if m == 0 else (gate1a[:, t0 : t0 + width] if t0 < HALF else gate1b[:, t0 - HALF : t0 - HALF + width])
+            h = min(n, 2)
+            g0 = t0 - GATES[h][0]
+            weight = gates[h][:, m, g0 : g0 + width]
             nc.vector.tensor_tensor(
                 windows[m][:].indirect(offsets[:, t0 // 16 : (t0 + width) // 16]), ys[n, m][:], weight, MULT
             )
@@ -128,16 +145,22 @@ def tile_picked_place_lin_gelu_srt_l_kernel(tc, xT, w_words, w_scales, b, gate, 
         quantize(0)
         quantize(1)
         activate(0)
-        scatter(0, 0)
         quantize(2)
+        scatter(0, 0)
         quantize(3)
-        activate(1)
         scatter(0, 1)
+        activate(1)
         quantize(4)
-        activate(2)
         scatter(1, 0)
-        scatter(2, 0)
-        nc.sync.dma_start(out=out[0:P, :], in_=windows[0][:])
+        quantize(5)
         scatter(1, 1)
+        quantize(6)
+        activate(2)
+        scatter(2, 0)
+        quantize(7)
+        activate(3)
+        scatter(3, 0)
+        nc.sync.dma_start(out=out[0:P, :], in_=windows[0][:])
         scatter(2, 1)
+        scatter(3, 1)
         nc.sync.dma_start(out=out[P:N, :], in_=windows[1][:])

@@ -22,17 +22,17 @@ PASSES = K // K_PASS
 M_TILES = N // P
 
 LOADS = (
-    (0, 0, 256, 128),
-    (1, 0, 256, 128),
-    (0, 256, 256, 32),
-    (1, 256, 256, 32),
-    (0, 512, 256, 32),
-    (1, 512, 256, 32),
-    (0, 768, 256, 32),
-    (1, 768, 256, 128),
+    (0, 0, 256, 144),
+    (1, 0, 256, 160),
+    (0, 256, 256, 64),
+    (1, 256, 256, 64),
+    (0, 512, 256, 64),
+    (1, 512, 256, 64),
+    (0, 768, 256, 64),
+    (1, 768, 256, 176),
 )
 BLOCKS = ((0, 256), (256, 256), (512, 256), (768, 256))
-GATES = ((0, 256), (256, 256), (512, 512))
+GATES = ((0, 2, 0, 256), (0, 2, 256, 256), (0, 1, 512, 512), (1, 1, 512, 512))
 
 
 def tile_picked_place_lin_gelu_srt_l_kernel(tc, xT, w_words, w_scales, b, gate, offs, out):
@@ -51,8 +51,8 @@ def tile_picked_place_lin_gelu_srt_l_kernel(tc, xT, w_words, w_scales, b, gate, 
             raw = keep.tile([P, PACK, width], F32, name=f"raw{i}", align_bytes=64)
             raws.append(raw)
         gates = []
-        for h, (t0, width) in enumerate(GATES):
-            gate_part = keep.tile([P, M_TILES, width], F32, name=f"gate{h}", align_bytes=64)
+        for h, (m0, tiles, t0, width) in enumerate(GATES):
+            gate_part = keep.tile([P, tiles, width], F32, name=f"gate{h}", align_bytes=64)
             gates.append(gate_part)
         nc.gpsimd.memset(w_planes[:].rearrange("p a n -> p (a n)").bitcast(I32), 0)
 
@@ -62,7 +62,8 @@ def tile_picked_place_lin_gelu_srt_l_kernel(tc, xT, w_words, w_scales, b, gate, 
             nc.sync.dma_start(out=raws[i][:], in_=rows.rearrange("(p j) w -> p j w", j=PACK))
 
         def load_gate(h):
-            cols = gate[:, GATES[h][0] : GATES[h][0] + GATES[h][1]]
+            m0, tiles, t0, width = GATES[h]
+            cols = gate[m0 * P : (m0 + tiles) * P, t0 : t0 + width]
             nc.sync.dma_start(out=gates[h][:], in_=cols.rearrange("(m p) w -> p m w", p=P))
 
         load_x(0)
@@ -78,14 +79,15 @@ def tile_picked_place_lin_gelu_srt_l_kernel(tc, xT, w_words, w_scales, b, gate, 
         load_x(1)
         nc.sync.dma_start(offsets[:], offs)
         load_gate(0)
+        load_gate(1)
         load_x(2)
         load_x(3)
-        load_gate(1)
         load_x(4)
         load_x(5)
         load_x(6)
         load_x(7)
         load_gate(2)
+        load_gate(3)
 
         nc.vector.memset(warm[:], 0.0)
         nc.scalar.activation(out=warmed[:], in_=warm[:], func=GELU)
@@ -135,9 +137,9 @@ def tile_picked_place_lin_gelu_srt_l_kernel(tc, xT, w_words, w_scales, b, gate, 
 
         def scatter(n, m):
             t0, width = BLOCKS[n]
-            h = min(n, 2)
-            g0 = t0 - GATES[h][0]
-            weight = gates[h][:, m, g0 : g0 + width]
+            for part, (m0, tiles, g0, g_width) in zip(gates, GATES):
+                if m0 <= m < m0 + tiles and g0 <= t0 < g0 + g_width:
+                    weight = part[:, m - m0, t0 - g0 : t0 - g0 + width]
             nc.vector.tensor_tensor(
                 windows[m][:].indirect(offsets[:, t0 // 16 : (t0 + width) // 16]), ys[n, m][:], weight, MULT
             )
@@ -145,22 +147,22 @@ def tile_picked_place_lin_gelu_srt_l_kernel(tc, xT, w_words, w_scales, b, gate, 
         quantize(0)
         quantize(1)
         activate(0)
-        quantize(2)
         scatter(0, 0)
-        quantize(3)
         scatter(0, 1)
+        quantize(2)
+        quantize(3)
         activate(1)
-        quantize(4)
         scatter(1, 0)
+        quantize(4)
         quantize(5)
-        scatter(1, 1)
-        quantize(6)
         activate(2)
-        scatter(2, 0)
+        quantize(6)
         quantize(7)
+        scatter(2, 0)
         activate(3)
         scatter(3, 0)
         nc.sync.dma_start(out=out[0:P, :], in_=windows[0][:])
+        scatter(1, 1)
         scatter(2, 1)
         scatter(3, 1)
         nc.sync.dma_start(out=out[P:N, :], in_=windows[1][:])

from contextlib import ExitStack

import concourse.mybir as mybir

K, S, N, T = 1024, 1024, 256, 2048
FLOPS = 2 * K * S * N

F32 = mybir.dt.float32
BF16 = mybir.dt.bfloat16
I32 = mybir.dt.int32
U32 = mybir.dt.uint32
U16 = mybir.dt.uint16
U8 = mybir.dt.uint8
FP8X4 = mybir.dt.float8_e4m3fn_x4
MULT = mybir.AluOpType.mult
GELU = mybir.ActivationFunctionType.Gelu_apprx_tanh

P = 128
PACK = 4
K_PASS = P * PACK
PASSES = K // K_PASS
M_TILES = N // P

LOADS = (
    (0, 0, 256, 144),
    (1, 0, 256, 160),
    (0, 256, 256, 64),
    (1, 256, 256, 64),
    (0, 512, 256, 64),
    (1, 512, 256, 64),
    (0, 768, 256, 64),
    (1, 768, 256, 176),
)
BLOCKS = ((0, 256), (256, 256), (512, 256), (768, 256))
GATES = ((0, 2, 0, 256), (0, 2, 256, 256), (0, 1, 512, 512), (1, 1, 512, 512))


def tile_picked_place_lin_gelu_srt_l_kernel(tc, xT, w_words, w_scales, b, gate, offs, out):
    nc = tc.nc
    with ExitStack() as ctx:
        keep = ctx.enter_context(tc.tile_pool(name="keep", bufs=1))
        psum = ctx.enter_context(tc.psum_pool(name="psum", bufs=1))

        offsets = keep.tile([P, S // 16], U16, name="offsets")
        w_codes = keep.tile([P, PASSES, N], U32, name="w_codes", align_bytes=64)
        w_planes = keep.tile([P, PASSES, N], U8, name="w_planes", align_bytes=64)
        warm = keep.tile([P, 1], F32, name="warm")
        warmed = keep.tile([P, 1], F32, name="warmed")
        raws = []
        for i, (k, t0, width, v) in enumerate(LOADS):
            raw = keep.tile([P, PACK, width], F32, name=f"raw{i}", align_bytes=64)
            raws.append(raw)
        gates = []
        for h, (m0, tiles, t0, width) in enumerate(GATES):
            gate_part = keep.tile([P, tiles, width], F32, name=f"gate{h}", align_bytes=64)
            gates.append(gate_part)
        nc.gpsimd.memset(w_planes[:].rearrange("p a n -> p (a n)").bitcast(I32), 0)

        def load_x(i):
            k, t0, width, v = LOADS[i]
            rows = xT[k * K_PASS : (k + 1) * K_PASS, t0 : t0 + width]
            nc.sync.dma_start(out=raws[i][:], in_=rows.rearrange("(p j) w -> p j w", j=PACK))

        def load_gate(h):
            m0, tiles, t0, width = GATES[h]
            cols = gate[m0 * P : (m0 + tiles) * P, t0 : t0 + width]
            nc.sync.dma_start(out=gates[h][:], in_=cols.rearrange("(m p) w -> p m w", p=P))

        load_x(0)
        for q in range(4):
            nc.scalar.dma_start(
                out=w_planes[32 * q : 32 * q + 4].bitcast(I32),
                in_=w_scales[:, 4 * q : 4 * q + 4, :].rearrange("a q n -> q a n").bitcast(I32),
            )
        bias = keep.tile([P, M_TILES], F32, name="bias")
        with nc.allow_non_contiguous_dma(reason="one bias value for each partition and output tile"):
            nc.scalar.dma_start(out=bias[:], in_=b.rearrange("(m p) o -> p (m o)", p=P))
        nc.sync.dma_start(out=w_codes[:].bitcast(I32), in_=w_words.rearrange("a p n r -> p a (n r)").bitcast(I32))
        load_x(1)
        nc.sync.dma_start(offsets[:], offs)
        load_gate(0)
        load_gate(1)
        load_x(2)
        load_x(3)
        load_x(4)
        load_x(5)
        load_x(6)
        load_x(7)
        load_gate(2)
        load_gate(3)

        nc.vector.memset(warm[:], 0.0)
        nc.scalar.activation(out=warmed[:], in_=warm[:], func=GELU)
        windows = []
        for m in range(M_TILES):
            window = keep.tile([P, T], F32, name=f"window{m}", align_bytes=64)
            nc.vector.memset(window[:], 0.0)
            windows.append(window)

        accs = {}
        ys = {}
        for n, (t0, width) in enumerate(BLOCKS):
            for m in range(M_TILES):
                accs[n, m] = psum.tile([P, width], F32, name=f"acc{n}_{m}")
                ys[n, m] = keep.tile([P, width], F32, name=f"y{n}_{m}", align_bytes=64)

        def quantize(i):
            k, t0, width, v = LOADS[i]
            grouped = keep.tile([P, width, PACK], BF16, name=f"grouped{i}", align_bytes=64)
            codes = keep.tile([P, width], U32, name=f"codes{i}", align_bytes=64)
            planes = keep.tile([P, width], U8, name=f"planes{i}", align_bytes=64)
            turned = raws[i][:].rearrange("p j (c i) -> p c j i", i=4)
            laid = grouped[:].rearrange("p (c i) j -> p c j i", i=4)
            nc.scalar.copy(out=laid[:, v // 4 :], in_=turned[:, v // 4 :])
            nc.vector.tensor_copy(out=laid[:, : v // 4], in_=turned[:, : v // 4])
            nc.vector.quantize_mx(
                out=codes[:].bitcast(FP8X4), scales=planes[:], in_=grouped[:].rearrange("p w j -> p (w j)")
            )
            for n, (b0, b_width) in enumerate(BLOCKS):
                if t0 <= b0 and b0 + b_width <= t0 + width:
                    cols = slice(b0 - t0, b0 - t0 + b_width)
                    for m in range(M_TILES):
                        m_cols = slice(m * P, (m + 1) * P)
                        nc.tensor.matmul_mx(
                            out=accs[n, m][:],
                            lhsT=w_codes[:, k, m_cols].bitcast(FP8X4),
                            lhsT_scale=w_planes[:, k, m_cols],
                            rhs=codes[:, cols].bitcast(FP8X4),
                            rhs_scale=planes[:, cols],
                            start=(k == 0),
                            stop=(k == PASSES - 1),
                        )

        def activate(n):
            for m in range(M_TILES):
                nc.scalar.activation(out=ys[n, m][:], in_=accs[n, m][:], func=GELU, bias=bias[:, m : m + 1])

        def scatter(n, m):
            t0, width = BLOCKS[n]
            for part, (m0, tiles, g0, g_width) in zip(gates, GATES):
                if m0 <= m < m0 + tiles and g0 <= t0 < g0 + g_width:
                    weight = part[:, m - m0, t0 - g0 : t0 - g0 + width]
            nc.vector.tensor_tensor(
                windows[m][:].indirect(offsets[:, t0 // 16 : (t0 + width) // 16]), ys[n, m][:], weight, MULT
            )

        quantize(0)
        quantize(1)
        activate(0)
        scatter(0, 0)
        scatter(0, 1)
        quantize(2)
        quantize(3)
        activate(1)
        scatter(1, 0)
        quantize(4)
        quantize(5)
        activate(2)
        quantize(6)
        quantize(7)
        scatter(2, 0)
        activate(3)
        scatter(3, 0)
        nc.sync.dma_start(out=out[0:P, :], in_=windows[0][:])
        scatter(1, 1)
        scatter(2, 1)
        scatter(3, 1)
        nc.sync.dma_start(out=out[P:N, :], in_=windows[1][:])
